import numpy as np
import ml_dtypes


def mxq(x, axis, fmt="e4m3"):
    dtype, down = {"e4m3": (ml_dtypes.float8_e4m3fn, 7), "e5m2": (ml_dtypes.float8_e5m2, 14)}[fmt]
    v = np.moveaxis(np.asarray(x, np.float32).astype(ml_dtypes.bfloat16).astype(np.float64), axis, -1)
    blocks = v.reshape(v.shape[:-1] + (-1, 32))
    amax = np.abs(blocks).max(-1, keepdims=True)
    byte = np.maximum(np.where(amax > 0, np.frexp(amax)[1] - 1 + 127, 0) - down, 1)
    scale = np.exp2(byte - 127.0)
    codes = (blocks / scale).astype(np.float32).astype(dtype).astype(np.float64)
    return np.moveaxis((codes * scale).reshape(v.shape), -1, axis)


WIDE = False


def mx_kscale(k):
    if not WIDE:
        return np.ones(k)
    levels = np.array([10, -10, 5, -5, 0])
    if k % 512:
        return np.exp2(np.random.permutation(np.resize(levels, k // 32))).repeat(32)
    a = np.empty((k // 512, 16))
    for p in range(k // 512):
        a[p, :8] = np.random.permutation(np.resize(levels, 8))
        for g in range(8):
            far = levels[np.abs(levels - a[p, g]) >= 10]
            a[p, g + 8] = far[np.random.randint(len(far))]
    return np.exp2(a.ravel()).repeat(32)


BF16 = ml_dtypes.bfloat16


def bf(x):
    return np.asarray(x, np.float32).astype(BF16)


def f64(x):
    return np.asarray(x).astype(np.float64)


E2M1 = np.array([0.0, 0.5, 1.0, 1.5, 2.0, 3.0, 4.0, 6.0, -0.0, -0.5, -1.0, -1.5, -2.0, -3.0, -4.0, -6.0])


def pack_weight(w, fmt):
    k, n = w.shape
    w = f64(bf(w)).reshape(k // 32, 32, n)
    amax = np.abs(w).max(1)
    if fmt == "e4m3":
        byte = np.frexp(amax)[1] - 1 + 127 - 7
    else:
        mant, ex = np.frexp(amax / 6.0)
        byte = np.where(mant > 0.5, ex, ex - 1) + 127
    byte = np.clip(np.where(amax > 0, byte, 1), 1, 254)
    scaled = (w * np.exp2(127.0 - byte)[:, None, :]).reshape(k, n).astype(np.float32)
    by_word = np.ascontiguousarray(scaled.reshape(k // 512, 128, 4, n).transpose(0, 1, 3, 2))
    if fmt == "e4m3":
        words = by_word.astype(ml_dtypes.float8_e4m3fn).view(np.uint8)
    else:
        c = by_word.astype(ml_dtypes.float4_e2m1fn).view(np.uint8) & 0xF
        words = c[..., 0::2] | (c[..., 1::2] << 4)
    return np.ascontiguousarray(words), np.ascontiguousarray(byte.astype(np.uint8).reshape(k // 512, 16, n))


def unpack_weight(words, scales, fmt):
    g, p, n, _ = words.shape
    if fmt == "e4m3":
        vals = np.ascontiguousarray(words).view(ml_dtypes.float8_e4m3fn).astype(np.float64)
    else:
        nib = np.empty((g, p, n, 4), np.uint8)
        nib[..., 0::2] = words & 0xF
        nib[..., 1::2] = words >> 4
        vals = E2M1[nib]
    vals = vals * np.repeat(np.exp2(scales.astype(np.float64) - 127.0), 8, axis=1)[..., None]
    return vals.transpose(0, 1, 3, 2).reshape(g * 512, n)
def pack4(w):
    words, scales = pack_weight(w, "e2m1")
    return words.reshape(words.shape[0], 128, -1), scales


def unpack4(words, scales):
    return unpack_weight(words.reshape(words.shape[0], 128, -1, 2), scales, "e2m1")


E4M3FN = np.array([(-1.0 if i & 128 else 1.0) * ((1.0 + (i & 7) / 8.0) * 2.0 ** (((i >> 3) & 15) - 7) if i & 120 else (i & 7) * 2.0 ** -9) for i in range(256)])


def e4m3fn_bytes(y):
    return np.clip(np.asarray(y, np.float64), -448.0, 448.0).astype(np.float32).astype(ml_dtypes.float8_e4m3fn).view(np.uint8)


def e4m3fn_values(b):
    return E4M3FN[b]


M, K, R, B = 1536, 1536, 1024, 128


def setup_inputs():
    s, t = mx_kscale(K), mx_kscale(R)
    grad = np.random.standard_normal((M, K)) * s
    grad_scale = (np.abs(grad).reshape(M, K // B, B).max(axis=2) / 448.0).astype(np.float32)
    grad_bytes = e4m3fn_bytes(grad / np.repeat(f64(grad_scale), B, axis=1))
    proj = np.random.standard_normal((K, R)) / np.sqrt(K) / s[:, None] * t
    back_words, back_scales = pack4(np.random.standard_normal((R, K)) / np.sqrt(R) / t[:, None])
    return {"grad_bytes": grad_bytes,
            "grad_scale": grad_scale,
            "proj": bf(proj),
            "mom": bf(0.5 * np.random.standard_normal((M, R)) * t),
            "pre": bf(0.5 + np.random.random((M, R))),
            "back_words": back_words,
            "back_scales": back_scales,
            "w": bf(0.5 * np.random.standard_normal((M, K))),
            "eta": bf(0.5 + 0.5 * np.random.random(M))}


def reference(grad_bytes, grad_scale, proj, mom, pre, back_words, back_scales, w, eta):
    grad = e4m3fn_values(grad_bytes) * np.repeat(f64(grad_scale), B, axis=1)
    low = mxq(grad, 1, "e4m3") @ mxq(f64(proj), 0, "e4m3")
    step = (low + f64(mom)) * f64(pre)
    upd = mxq(step, 1, "e4m3") @ unpack4(back_words, back_scales)
    return f64(w) - upd * f64(eta)[:, None]

@@ -1,0 +1,393 @@
+from contextlib import ExitStack
+
+import concourse.mybir as mybir
+from concourse.masks import make_identity
+
+M, K, R = 1536, 1536, 1024
+FLOPS = 2 * M * K * R * 2
+
+F32 = mybir.dt.float32
+BF16 = mybir.dt.bfloat16
+I32 = mybir.dt.int32
+U32 = mybir.dt.uint32
+U8 = mybir.dt.uint8
+FP8 = mybir.dt.float8_e4m3fn
+FP8X4 = mybir.dt.float8_e4m3fn_x4
+FP4X4 = mybir.dt.float4_e2m1fn_x4
+ALU = mybir.AluOpType
+COPY = mybir.ActivationFunctionType.Copy
+
+P = 128
+PACK = 4
+PASS = P * PACK
+BANK = 512
+TILES = M // P
+K_PASSES = K // PASS
+R_PASSES = R // PASS
+K_BLOCKS = K // P
+K_BANKS = K // BANK
+PAIR = 2
+WARM = 6
+
+GRAD_BANKS = (0, 1)
+STEP_BANK = 2
+LOW_BANKS = (3, 4)
+UPD_BANKS = (5, 6, 7)
+PROJ_BANKS = (5, 6, 7, 2)
+
+
+def tile_fp8_gradient_projection_d4_kernel(
+    tc, grad_bytes, grad_scale, proj, mom, pre, back_words, back_scales, w, eta, out
+):
+    nc = tc.nc
+    grad_rows = grad_bytes.rearrange("(p i) k -> p i k", i=TILES)
+    mom_rows = mom.rearrange("(p i) r -> p i r", i=TILES)
+    pre_rows = pre.rearrange("(p i) r -> p i r", i=TILES)
+    w_rows = w.rearrange("(p i) k -> p i k", i=TILES)
+    out_rows = out.rearrange("(p i) k -> p i k", i=TILES)
+    proj_rows = proj.rearrange("(g p t) r -> g p t r", p=P, t=PACK)
+
+    with ExitStack() as ctx:
+        keep = ctx.enter_context(tc.tile_pool(name="keep", bufs=1))
+        work = ctx.enter_context(tc.tile_pool(name="work", bufs=3))
+        psum = ctx.enter_context(tc.psum_pool(name="psum", bufs=1))
+        ctx.enter_context(tc.manual_schedule())
+
+        def bank(index, dtype=F32):
+            width = BANK if dtype == F32 else 2 * BANK
+            return psum.tile([P, width], dtype, name="bank%d" % index, tag="bank%d" % index)
+
+        grad_raw, mom_sb, pre_sb, w_sb, proj_raw = {}, {}, {}, {}, {}
+        grad_wide, grad_banks, grad_grouped, grad_q = {}, {}, {}, {}
+        low_banks, total, step, step_bank, step_grouped, step_q = {}, {}, {}, {}, {}, {}
+        upd_banks, proj_grouped, result = {}, {}, {}
+
+        def load_rows(store, rows, first, count, width, dtype, label):
+            sb = keep.tile([P, count, width], dtype, name="%s%d" % (label, first), align_bytes=64)
+            nc.sync.dma_start(out=sb[:], in_=rows[:, first : first + count, :])
+            for j in range(count):
+                store[first + j] = sb[:, j, :]
+
+        def load_grad(first, count):
+            load_rows(grad_raw, grad_rows, first, count, K, U8, "grad_raw")
+
+        def load_mom_pre(first, count):
+            load_rows(mom_sb, mom_rows, first, count, R, BF16, "mom_sb")
+            load_rows(pre_sb, pre_rows, first, count, R, BF16, "pre_sb")
+
+        def load_w(first, count):
+            load_rows(w_sb, w_rows, first, count, K, BF16, "w_sb")
+
+        def load_proj(g, pieces=1):
+            width = R // pieces
+            for n in range(pieces):
+                raw = keep.tile([P, PACK, width], BF16, name="proj_raw%d_%d" % (g, n), align_bytes=64)
+                nc.sync.dma_start(out=raw[:], in_=proj_rows[g][:, :, n * width : (n + 1) * width])
+                for c in range(width // P):
+                    proj_raw[g, n * width // P + c] = raw[:, :, c * P : (c + 1) * P]
+
+        scale_sb = keep.tile([P, TILES * K_BLOCKS], F32, name="scale_sb")
+        nc.sync.dma_start(out=scale_sb[:], in_=grad_scale.rearrange("(p i) j -> p (i j)", i=TILES))
+        load_grad(0, 1)
+        load_grad(1, 1)
+        load_proj(0)
+        load_proj(1)
+        load_proj(2, 2)
+        load_mom_pre(0, 1)
+        load_grad(2, 1)
+        load_mom_pre(1, 1)
+
+        ident_bf = keep.tile([P, P], BF16, name="ident_bf", align_bytes=64)
+        make_identity(nc, ident_bf[:])
+        ident_f32 = keep.tile([P, P], F32, name="ident_f32", align_bytes=64)
+        make_identity(nc, ident_f32[:])
+        back_sc = keep.tile([P, R_PASSES, K], U8, name="back_sc", align_bytes=64)
+        nc.gpsimd.memset(back_sc[:].rearrange("p g n -> p (g n)").bitcast(I32), 0)
+        table_warm = keep.tile([P, 1], F32, name="table_warm")
+        nc.scalar.activation(out=table_warm[:], in_=ident_f32[:, 0:1], func=COPY, scale=ident_f32[:, 1:2])
+
+        back_codes = keep.tile([P, R_PASSES, 2 * K], U8, name="back_codes", align_bytes=64)
+        nc.sync.dma_start(
+            out=back_codes[:].bitcast(I32), in_=back_words.rearrange("g p n -> p g n").bitcast(I32)
+        )
+        for q in range(4):
+            nc.sync.dma_start(
+                out=back_sc[32 * q : 32 * q + 4, :, :].bitcast(I32),
+                in_=back_scales[:, 4 * q : 4 * q + 4, :].rearrange("g q n -> q g n").bitcast(I32),
+            )
+        eta_sb = keep.tile([P, TILES], BF16, name="eta_sb")
+        nc.sync.dma_start(out=eta_sb[:], in_=eta.rearrange("(p i) -> p i", i=TILES))
+        load_grad(3, 1)
+        load_w(0, 1)
+        load_mom_pre(2, 1)
+        load_grad(4, 2)
+        load_w(1, 1)
+        load_mom_pre(3, 1)
+        load_w(2, 2)
+
+        proj_codes = keep.tile([P, K_PASSES, R], U32, name="proj_codes", align_bytes=64)
+        proj_scales = keep.tile([P, K_PASSES, R], U8, name="proj_scales", align_bytes=64)
+
+        def widen(i, on_vector=False):
+            wide = work.tile([P, K], BF16, name="grad_wide", tag="grad_wide", bufs=2, align_bytes=64)
+            for j in range(K_BLOCKS):
+                cols = slice(j * P, (j + 1) * P)
+                factor = scale_sb[:, i * K_BLOCKS + j : i * K_BLOCKS + j + 1]
+                src = grad_raw[i][:, cols].bitcast(FP8)
+                if on_vector:
+                    nc.vector.tensor_scalar(
+                        out=wide[:, cols], in0=src, scalar1=factor, scalar2=None, op0=ALU.mult
+                    )
+                else:
+                    nc.scalar.activation(out=wide[:, cols], in_=src, func=COPY, scale=factor)
+            grad_wide[i] = wide
+
+        def turn_grad(i, where=GRAD_BANKS):
+            words = grad_wide[i][:].bitcast(F32)
+            banks = [bank(b) for b in where]
+            for g in range(K_PASSES):
+                for u in range(2):
+                    at = (2 * (g % 2) + u) * P
+                    nc.tensor.transpose(
+                        banks[g // 2][:, at : at + P],
+                        words[:, 2 * P * g + u : 2 * P * (g + 1) : 2],
+                        ident_f32[:],
+                    )
+            grad_banks[i] = banks
+
+        def empty_grad(i, on_vector=False):
+            copy = nc.vector.tensor_copy if on_vector else nc.scalar.copy
+            grouped = work.tile([P, K], BF16, name="grad_grouped", tag="grad_grouped", bufs=2, align_bytes=64)
+            words = grouped[:].bitcast(F32)
+            first, second = grad_banks[i]
+            copy(
+                out=words[:, 0 : 4 * P].rearrange("p (g m u) -> p g m u", g=2, u=2),
+                in_=first[:].rearrange("p (g u m) -> p g m u", g=2, u=2),
+            )
+            copy(
+                out=words[:, 4 * P : 6 * P].rearrange("p (m u) -> p m u", u=2),
+                in_=second[:, 0 : 2 * P].rearrange("p (u m) -> p m u", u=2),
+            )
+            grad_grouped[i] = grouped
+
+        def quantize_grad(i):
+            codes = work.tile([P, K_PASSES * P], U32, name="grad_codes", tag="grad_codes", align_bytes=64)
+            scales = work.tile([P, K_PASSES * P], U8, name="grad_scales", tag="grad_scales", align_bytes=64)
+            for lo, hi in ((0, 2 * P), (2 * P, 3 * P)):
+                nc.vector.quantize_mx(
+                    out=codes[:, lo:hi].bitcast(FP8X4),
+                    scales=scales[:, lo:hi],
+                    in_=grad_grouped[i][:, PACK * lo : PACK * hi],
+                )
+            grad_q[i] = (codes, scales)
+
+        def interleave_proj(g, quarter, on_vector=False):
+            if quarter == 0:
+                proj_grouped[g] = work.tile(
+                    [P, PACK * R], BF16, name="proj_grouped", tag="proj_grouped", bufs=2, align_bytes=64
+                )
+            dst = proj_grouped[g][:, quarter * 2 * BANK : (quarter + 1) * 2 * BANK]
+            if on_vector:
+                for half in range(2):
+                    nc.vector.tensor_copy(
+                        out=dst[:, half * BANK : (half + 1) * BANK].rearrange("p (c t) -> p c t", t=PACK),
+                        in_=proj_raw[g, 2 * quarter + half].rearrange("p t c -> p c t"),
+                    )
+                return
+            acc = bank(PROJ_BANKS[quarter], BF16)
+            for half in range(2):
+                nc.tensor.matmul(
+                    acc[:, half * BANK : (half + 1) * BANK],
+                    lhsT=ident_bf[:],
+                    rhs=proj_raw[g, 2 * quarter + half].rearrange("p t c -> p c t"),
+                    start=True,
+                    stop=True,
+                )
+            nc.scalar.copy(out=dst, in_=acc[:])
+
+        def quantize_proj(g, first, count):
+            cols = slice(first * 2 * P, (first + count) * 2 * P)
+            nc.vector.quantize_mx(
+                out=proj_codes[:, g, cols].bitcast(FP8X4),
+                scales=proj_scales[:, g, cols],
+                in_=proj_grouped[g][:, PACK * cols.start : PACK * cols.stop],
+            )
+
+        def low_pass(i, h, g):
+            codes, scales = grad_q[i]
+            nc.tensor.matmul_mx(
+                out=low_banks[i][h][:],
+                lhsT=codes[:, g * P : (g + 1) * P].bitcast(FP8X4),
+                lhsT_scale=scales[:, g * P : (g + 1) * P],
+                rhs=proj_codes[:, g, h * BANK : (h + 1) * BANK].bitcast(FP8X4),
+                rhs_scale=proj_scales[:, g, h * BANK : (h + 1) * BANK],
+                start=(g == 0),
+                stop=(g == K_PASSES - 1),
+            )
+
+        def multiply_low(i, banks=LOW_BANKS):
+            low_banks[i] = [bank(b) for b in banks]
+            for h in range(R_PASSES):
+                for g in range(K_PASSES):
+                    low_pass(i, h, g)
+
+        def add_mom(i, h):
+            if h == 0:
+                total[i] = work.tile([P, R], F32, name="total", tag="total", bufs=2, align_bytes=64)
+            cols = slice(h * BANK, (h + 1) * BANK)
+            nc.vector.tensor_tensor(out=total[i][:, cols], in0=low_banks[i][h][:], in1=mom_sb[i][:, cols], op=ALU.add)
+
+        def precondition(i, h):
+            if h == 0:
+                step[i] = work.tile([P, R], BF16, name="step", tag="step", align_bytes=64)
+            cols = slice(h * BANK, (h + 1) * BANK)
+            nc.vector.tensor_tensor(
+                out=step[i][:, cols].rearrange("p (u c e) -> p u c e", u=2, e=2),
+                in0=total[i][:, cols].rearrange("p (c u e) -> p u c e", u=2, e=2),
+                in1=pre_sb[i][:, cols].rearrange("p (c u e) -> p u c e", u=2, e=2),
+                op=ALU.mult,
+            )
+
+        def turn_step(i):
+            words = step[i][:].bitcast(F32)
+            acc = bank(STEP_BANK)
+            for n in range(4):
+                nc.tensor.transpose(acc[:, n * P : (n + 1) * P], words[:, n * P : (n + 1) * P], ident_f32[:])
+            step_bank[i] = acc
+
+        def empty_step(i):
+            grouped = work.tile([P, R], BF16, name="step_grouped", tag="step_grouped", bufs=2, align_bytes=64)
+            nc.scalar.copy(
+                out=grouped[:].bitcast(F32).rearrange("p (h m u) -> p h m u", h=2, u=2),
+                in_=step_bank[i][:].rearrange("p (h u m) -> p h m u", h=2, u=2),
+            )
+            step_grouped[i] = grouped
+
+        def quantize_step(i):
+            codes = work.tile([P, R_PASSES * P], U32, name="step_codes", tag="step_codes", align_bytes=64)
+            scales = work.tile([P, R_PASSES * P], U8, name="step_scales", tag="step_scales", align_bytes=64)
+            nc.vector.quantize_mx(out=codes[:].bitcast(FP8X4), scales=scales[:], in_=step_grouped[i][:])
+            step_q[i] = (codes, scales)
+
+        def multiply_upd(i):
+            codes, scales = step_q[i]
+            upd_banks[i] = [bank(b) for b in UPD_BANKS]
+            for n in range(K_BANKS):
+                for h in range(R_PASSES):
+                    nc.tensor.matmul_mx(
+                        out=upd_banks[i][n][:],
+                        lhsT=codes[:, h * P : (h + 1) * P].bitcast(FP8X4),
+                        lhsT_scale=scales[:, h * P : (h + 1) * P],
+                        rhs=back_codes[:, h, 2 * n * BANK : 2 * (n + 1) * BANK].bitcast(FP4X4),
+                        rhs_scale=back_sc[:, h, n * BANK : (n + 1) * BANK],
+                        start=(h == 0),
+                        stop=(h == R_PASSES - 1),
+                    )
+
+        def update(i):
+            result[i] = work.tile([P, K], F32, name="result", tag="result", bufs=3, align_bytes=64)
+            for n in range(K_BANKS):
+                cols = slice(n * BANK, (n + 1) * BANK)
+                nc.vector.scalar_tensor_tensor(
+                    out=result[i][:, cols],
+                    in0=upd_banks[i][n][:],
+                    scalar=neg_eta[:, i : i + 1],
+                    in1=w_sb[i][:, cols],
+                    op0=ALU.mult,
+                    op1=ALU.add,
+                )
+                if i >= TILES - 2:
+                    nc.sync.dma_start(out=out_rows[:, i, cols], in_=result[i][:, cols])
+            if i < TILES - 2:
+                nc.sync.dma_start(out=out_rows[:, i, :], in_=result[i][:])
+
+        warm_in = keep.tile([P, BANK], BF16, name="warm_in", align_bytes=64)
+        nc.vector.memset(warm_in[:], 0.0)
+        warm = bank(LOW_BANKS[0])
+        for n in range(WARM):
+            nc.tensor.matmul(warm[:], lhsT=ident_bf[:], rhs=warm_in[:], start=True, stop=True)
+        widen(0, True)
+        turn_grad(0)
+        empty_grad(0)
+        widen(1, True)
+        turn_grad(1, LOW_BANKS)
+        interleave_proj(0, 0)
+        interleave_proj(0, 1)
+        interleave_proj(0, 2)
+        quantize_grad(0)
+        empty_grad(1, True)
+        interleave_proj(0, 3, True)
+        quantize_proj(0, 0, 2)
+        quantize_grad(1)
+        quantize_proj(0, 2, 2)
+        interleave_proj(1, 0)
+        interleave_proj(1, 1)
+        interleave_proj(1, 2)
+        interleave_proj(1, 3, True)
+        quantize_proj(1, 0, 2)
+        quantize_proj(1, 2, 2)
+        low_banks[0] = [bank(b) for b in LOW_BANKS]
+        low_pass(0, 0, 0)
+        low_pass(0, 1, 0)
+        interleave_proj(2, 0)
+        interleave_proj(2, 1)
+        interleave_proj(2, 2)
+        low_pass(0, 0, 1)
+        low_pass(0, 1, 1)
+        quantize_proj(2, 0, 2)
+        interleave_proj(2, 3, True)
+        quantize_proj(2, 2, 1)
+        quantize_proj(2, 3, 1)
+        low_pass(0, 0, 2)
+        low_pass(0, 1, 2)
+        widen(2)
+        multiply_low(1, banks=UPD_BANKS[0:2])
+        add_mom(0, 0)
+        add_mom(0, 1)
+        precondition(0, 0)
+        precondition(0, 1)
+        turn_grad(2)
+        turn_step(0)
+        empty_step(0)
+        empty_grad(2)
+        widen(3)
+        add_mom(1, 0)
+        add_mom(1, 1)
+        precondition(1, 0)
+        quantize_step(0)
+        precondition(1, 1)
+        quantize_grad(2)
+        neg_eta = keep.tile([P, TILES], F32, name="neg_eta")
+        nc.vector.tensor_scalar(out=neg_eta[:], in0=eta_sb[:], scalar1=-1.0, scalar2=None, op0=ALU.mult)
+        multiply_upd(0)
+
+        for s in range(2, TILES + 2):
+            if s % PAIR == 0 and s + PAIR < TILES:
+                load_mom_pre(s + PAIR, PAIR)
+                if s + 2 * PAIR < TILES:
+                    load_grad(s + 2 * PAIR, PAIR)
+                load_w(s + PAIR, PAIR)
+            if s + 1 < TILES:
+                turn_grad(s + 1)
+            if s - 1 < TILES:
+                turn_step(s - 1)
+            update(s - 2)
+            if s - 1 < TILES:
+                empty_step(s - 1)
+            if s + 1 < TILES:
+                empty_grad(s + 1)
+            if s - 1 < TILES:
+                quantize_step(s - 1)
+            if s < TILES:
+                multiply_low(s)
+                add_mom(s, 0)
+            if s + 1 < TILES:
+                quantize_grad(s + 1)
+            if s < TILES:
+                add_mom(s, 1)
+                precondition(s, 0)
+                precondition(s, 1)
+            if s - 1 < TILES:
+                multiply_upd(s - 1)
+            if s + 2 < TILES:
+                widen(s + 2)

@@ -27,7 +27,7 @@ R_PASSES = R // PASS
 K_BLOCKS = K // P
 K_BANKS = K // BANK
 PAIR = 2
-WARM = 6
+WARM = 16
 
 GRAD_BANKS = (0, 1)
 STEP_BANK = 2
@@ -89,13 +89,17 @@ def tile_fp8_gradient_projection_d4_kernel(
         scale_sb = keep.tile([P, TILES * K_BLOCKS], F32, name="scale_sb")
         nc.sync.dma_start(out=scale_sb[:], in_=grad_scale.rearrange("(p i) j -> p (i j)", i=TILES))
         load_grad(0, 1)
-        load_grad(1, 1)
+        load_grad(1, 2)
         load_proj(0)
         load_proj(1)
         load_proj(2, 2)
+        load_grad(3, 1)
+        eta_sb = keep.tile([P, TILES], BF16, name="eta_sb")
+        nc.sync.dma_start(out=eta_sb[:], in_=eta.rearrange("(p i) -> p i", i=TILES))
         load_mom_pre(0, 1)
-        load_grad(2, 1)
         load_mom_pre(1, 1)
+        load_grad(4, 2)
+        load_mom_pre(2, 1)
 
         ident_bf = keep.tile([P, P], BF16, name="ident_bf", align_bytes=64)
         make_identity(nc, ident_bf[:])
@@ -115,21 +119,18 @@ def tile_fp8_gradient_projection_d4_kernel(
                 out=back_sc[32 * q : 32 * q + 4, :, :].bitcast(I32),
                 in_=back_scales[:, 4 * q : 4 * q + 4, :].rearrange("g q n -> q g n").bitcast(I32),
             )
-        eta_sb = keep.tile([P, TILES], BF16, name="eta_sb")
-        nc.sync.dma_start(out=eta_sb[:], in_=eta.rearrange("(p i) -> p i", i=TILES))
-        load_grad(3, 1)
         load_w(0, 1)
-        load_mom_pre(2, 1)
-        load_grad(4, 2)
-        load_w(1, 1)
         load_mom_pre(3, 1)
+        load_grad(6, 2)
+        load_w(1, 1)
+        load_mom_pre(4, 2)
         load_w(2, 2)
 
         proj_codes = keep.tile([P, K_PASSES, R], U32, name="proj_codes", align_bytes=64)
         proj_scales = keep.tile([P, K_PASSES, R], U8, name="proj_scales", align_bytes=64)
 
         def widen(i, on_vector=False):
-            wide = work.tile([P, K], BF16, name="grad_wide", tag="grad_wide", bufs=2, align_bytes=64)
+            wide = work.tile([P, K], BF16, name="grad_wide", tag="grad_wide", align_bytes=64)
             for j in range(K_BLOCKS):
                 cols = slice(j * P, (j + 1) * P)
                 factor = scale_sb[:, i * K_BLOCKS + j : i * K_BLOCKS + j + 1]
@@ -157,7 +158,7 @@ def tile_fp8_gradient_projection_d4_kernel(
 
         def empty_grad(i, on_vector=False):
             copy = nc.vector.tensor_copy if on_vector else nc.scalar.copy
-            grouped = work.tile([P, K], BF16, name="grad_grouped", tag="grad_grouped", bufs=2, align_bytes=64)
+            grouped = work.tile([P, K], BF16, name="grad_grouped", tag="grad_grouped", align_bytes=64)
             words = grouped[:].bitcast(F32)
             first, second = grad_banks[i]
             copy(
@@ -237,20 +238,20 @@ def tile_fp8_gradient_projection_d4_kernel(
             cols = slice(h * BANK, (h + 1) * BANK)
             nc.vector.tensor_tensor(out=total[i][:, cols], in0=low_banks[i][h][:], in1=mom_sb[i][:, cols], op=ALU.add)
 
-        def precondition(i, h):
+        def precondition(i, h, engine):
             if h == 0:
                 step[i] = work.tile([P, R], BF16, name="step", tag="step", align_bytes=64)
             cols = slice(h * BANK, (h + 1) * BANK)
-            nc.vector.tensor_tensor(
+            engine.tensor_tensor(
                 out=step[i][:, cols].rearrange("p (u c e) -> p u c e", u=2, e=2),
                 in0=total[i][:, cols].rearrange("p (c u e) -> p u c e", u=2, e=2),
                 in1=pre_sb[i][:, cols].rearrange("p (c u e) -> p u c e", u=2, e=2),
                 op=ALU.mult,
             )
 
-        def turn_step(i):
+        def turn_step(i, where=STEP_BANK):
             words = step[i][:].bitcast(F32)
-            acc = bank(STEP_BANK)
+            acc = bank(where)
             for n in range(4):
                 nc.tensor.transpose(acc[:, n * P : (n + 1) * P], words[:, n * P : (n + 1) * P], ident_f32[:])
             step_bank[i] = acc
@@ -269,9 +270,9 @@ def tile_fp8_gradient_projection_d4_kernel(
             nc.vector.quantize_mx(out=codes[:].bitcast(FP8X4), scales=scales[:], in_=step_grouped[i][:])
             step_q[i] = (codes, scales)
 
-        def multiply_upd(i):
+        def multiply_upd(i, banks=UPD_BANKS):
             codes, scales = step_q[i]
-            upd_banks[i] = [bank(b) for b in UPD_BANKS]
+            upd_banks[i] = [bank(b) for b in banks]
             for n in range(K_BANKS):
                 for h in range(R_PASSES):
                     nc.tensor.matmul_mx(
@@ -284,38 +285,39 @@ def tile_fp8_gradient_projection_d4_kernel(
                         stop=(h == R_PASSES - 1),
                     )
 
-        def update(i):
-            result[i] = work.tile([P, K], F32, name="result", tag="result", bufs=3, align_bytes=64)
-            for n in range(K_BANKS):
-                cols = slice(n * BANK, (n + 1) * BANK)
-                nc.vector.scalar_tensor_tensor(
-                    out=result[i][:, cols],
-                    in0=upd_banks[i][n][:],
-                    scalar=neg_eta[:, i : i + 1],
-                    in1=w_sb[i][:, cols],
-                    op0=ALU.mult,
-                    op1=ALU.add,
-                )
-                if i >= TILES - 2:
-                    nc.sync.dma_start(out=out_rows[:, i, cols], in_=result[i][:, cols])
-            if i < TILES - 2:
+        def update(i, n):
+            if n == 0:
+                result[i] = work.tile([P, K], F32, name="result", tag="result", bufs=3, align_bytes=64)
+            cols = slice(n * BANK, (n + 1) * BANK)
+            nc.vector.scalar_tensor_tensor(
+                out=result[i][:, cols],
+                in0=upd_banks[i][n][:],
+                scalar=neg_eta[:, i : i + 1],
+                in1=w_sb[i][:, cols],
+                op0=ALU.mult,
+                op1=ALU.add,
+            )
+            if i >= TILES - 2:
+                nc.sync.dma_start(out=out_rows[:, i, cols], in_=result[i][:, cols])
+            elif n == K_BANKS - 1:
                 nc.sync.dma_start(out=out_rows[:, i, :], in_=result[i][:])
 
-        warm_in = keep.tile([P, BANK], BF16, name="warm_in", align_bytes=64)
-        nc.vector.memset(warm_in[:], 0.0)
         warm = bank(LOW_BANKS[0])
         for n in range(WARM):
-            nc.tensor.matmul(warm[:], lhsT=ident_bf[:], rhs=warm_in[:], start=True, stop=True)
+            nc.tensor.matmul(warm[:, 0:P], lhsT=ident_bf[:], rhs=ident_bf[:], start=True, stop=True)
+        neg_eta = keep.tile([P, TILES], F32, name="neg_eta")
         widen(0, True)
         turn_grad(0)
         empty_grad(0)
         widen(1, True)
         turn_grad(1, LOW_BANKS)
+        widen(2, True)
         interleave_proj(0, 0)
+        empty_grad(1)
         interleave_proj(0, 1)
         interleave_proj(0, 2)
+        turn_grad(2)
         quantize_grad(0)
-        empty_grad(1, True)
         interleave_proj(0, 3, True)
         quantize_proj(0, 0, 2)
         quantize_grad(1)
@@ -323,6 +325,7 @@ def tile_fp8_gradient_projection_d4_kernel(
         interleave_proj(1, 0)
         interleave_proj(1, 1)
         interleave_proj(1, 2)
+        empty_grad(2)
         interleave_proj(1, 3, True)
         quantize_proj(1, 0, 2)
         quantize_proj(1, 2, 2)
@@ -334,60 +337,69 @@ def tile_fp8_gradient_projection_d4_kernel(
         interleave_proj(2, 2)
         low_pass(0, 0, 1)
         low_pass(0, 1, 1)
-        quantize_proj(2, 0, 2)
         interleave_proj(2, 3, True)
+        quantize_proj(2, 0, 2)
         quantize_proj(2, 2, 1)
         quantize_proj(2, 3, 1)
         low_pass(0, 0, 2)
         low_pass(0, 1, 2)
-        widen(2)
-        multiply_low(1, banks=UPD_BANKS[0:2])
+        widen(3)
+        multiply_low(1, UPD_BANKS[0:2])
         add_mom(0, 0)
         add_mom(0, 1)
-        precondition(0, 0)
-        precondition(0, 1)
-        turn_grad(2)
-        turn_step(0)
-        empty_step(0)
-        empty_grad(2)
-        widen(3)
+        precondition(0, 0, nc.vector)
+        quantize_grad(2)
+        precondition(0, 1, nc.vector)
+        widen(4)
+        turn_grad(3)
+        empty_grad(3)
         add_mom(1, 0)
         add_mom(1, 1)
-        precondition(1, 0)
-        quantize_step(0)
-        precondition(1, 1)
-        quantize_grad(2)
-        neg_eta = keep.tile([P, TILES], F32, name="neg_eta")
         nc.vector.tensor_scalar(out=neg_eta[:], in0=eta_sb[:], scalar1=-1.0, scalar2=None, op0=ALU.mult)
-        multiply_upd(0)
+        precondition(1, 0, nc.vector)
+        precondition(1, 1, nc.vector)
 
-        for s in range(2, TILES + 2):
-            if s % PAIR == 0 and s + PAIR < TILES:
-                load_mom_pre(s + PAIR, PAIR)
-                if s + 2 * PAIR < TILES:
-                    load_grad(s + 2 * PAIR, PAIR)
-                load_w(s + PAIR, PAIR)
-            if s + 1 < TILES:
-                turn_grad(s + 1)
-            if s - 1 < TILES:
-                turn_step(s - 1)
-            update(s - 2)
-            if s - 1 < TILES:
-                empty_step(s - 1)
-            if s + 1 < TILES:
-                empty_grad(s + 1)
-            if s - 1 < TILES:
-                quantize_step(s - 1)
-            if s < TILES:
-                multiply_low(s)
-                add_mom(s, 0)
+        for s in range(2, TILES):
+            if s % PAIR == 0 and s >= 4:
+                if s + 2 < TILES:
+                    load_mom_pre(s + 2, PAIR)
+                if s + 4 < TILES:
+                    load_grad(s + 4, PAIR)
+                load_w(s, PAIR)
+            if s + 2 < TILES:
+                turn_grad(s + 2)
+            turn_step(s - 2)
+            empty_step(s - 2)
+            if s + 2 < TILES:
+                empty_grad(s + 2)
+            if s + 3 < TILES:
+                widen(s + 3)
+            if s >= 3:
+                update(s - 3, 2)
             if s + 1 < TILES:
                 quantize_grad(s + 1)
-            if s < TILES:
-                add_mom(s, 1)
-                precondition(s, 0)
-                precondition(s, 1)
-            if s - 1 < TILES:
-                multiply_upd(s - 1)
-            if s + 2 < TILES:
-                widen(s + 2)
+            quantize_step(s - 2)
+            multiply_low(s)
+            add_mom(s, 0)
+            precondition(s, 0, nc.gpsimd)
+            add_mom(s, 1)
+            precondition(s, 1, nc.gpsimd)
+            if s == TILES - 1:
+                turn_step(s - 1)
+                empty_step(s - 1)
+            multiply_upd(s - 2)
+            update(s - 2, 0)
+            update(s - 2, 1)
+        update(TILES - 3, 2)
+        quantize_step(TILES - 2)
+        turn_step(TILES - 1)
+        empty_step(TILES - 1)
+        multiply_upd(TILES - 2, LOW_BANKS + GRAD_BANKS[0:1])
+        update(TILES - 2, 0)
+        quantize_step(TILES - 1)
+        multiply_upd(TILES - 1)
+        update(TILES - 2, 1)
+        update(TILES - 2, 2)
+        update(TILES - 1, 0)
+        update(TILES - 1, 1)
+        update(TILES - 1, 2)

@@ -27,13 +27,13 @@ R_PASSES = R // PASS
 K_BLOCKS = K // P
 K_BANKS = K // BANK
 PAIR = 2
+QUARTER = R // 4
 WARM = 16
 
 GRAD_BANKS = (0, 1)
 STEP_BANK = 2
 LOW_BANKS = (3, 4)
 UPD_BANKS = (5, 6, 7)
-PROJ_BANKS = (5, 6, 7, 2)
 
 
 def tile_fp8_gradient_projection_d4_kernel(
@@ -60,7 +60,7 @@ def tile_fp8_gradient_projection_d4_kernel(
         grad_raw, mom_sb, pre_sb, w_sb, proj_raw = {}, {}, {}, {}, {}
         grad_wide, grad_banks, grad_grouped, grad_q = {}, {}, {}, {}
         low_banks, total, step, step_bank, step_grouped, step_q = {}, {}, {}, {}, {}, {}
-        upd_banks, proj_grouped, result = {}, {}, {}
+        upd_banks, proj_grouped, result, grad_halves = {}, {}, {}, {}
 
         def load_rows(store, rows, first, count, width, dtype, label):
             sb = keep.tile([P, count, width], dtype, name="%s%d" % (label, first), align_bytes=64)
@@ -83,17 +83,17 @@ def tile_fp8_gradient_projection_d4_kernel(
             for n in range(pieces):
                 raw = keep.tile([P, PACK, width], BF16, name="proj_raw%d_%d" % (g, n), align_bytes=64)
                 nc.sync.dma_start(out=raw[:], in_=proj_rows[g][:, :, n * width : (n + 1) * width])
-                for c in range(width // P):
-                    proj_raw[g, n * width // P + c] = raw[:, :, c * P : (c + 1) * P]
+                for c in range(width // QUARTER):
+                    proj_raw[g, n * width // QUARTER + c] = raw[:, :, c * QUARTER : (c + 1) * QUARTER]
 
         scale_sb = keep.tile([P, TILES * K_BLOCKS], F32, name="scale_sb")
         nc.sync.dma_start(out=scale_sb[:], in_=grad_scale.rearrange("(p i) j -> p (i j)", i=TILES))
         load_grad(0, 1)
-        load_grad(1, 2)
-        load_proj(0)
+        load_proj(0, 2)
+        load_grad(1, 1)
         load_proj(1)
-        load_proj(2, 2)
-        load_grad(3, 1)
+        load_proj(2)
+        load_grad(2, 2)
         eta_sb = keep.tile([P, TILES], BF16, name="eta_sb")
         nc.sync.dma_start(out=eta_sb[:], in_=eta.rearrange("(p i) -> p i", i=TILES))
         load_mom_pre(0, 1)
@@ -143,15 +143,28 @@ def tile_fp8_gradient_projection_d4_kernel(
                     nc.scalar.activation(out=wide[:, cols], in_=src, func=COPY, scale=factor)
             grad_wide[i] = wide
 
+        def split_words(i, on_vector=False):
+            halves = work.tile([P, K // 2], F32, name="grad_halves", tag="grad_halves", bufs=2, align_bytes=64)
+            copy = nc.vector.tensor_copy if on_vector else nc.scalar.copy
+            copy(
+                out=halves[:].rearrange("p (g u c) -> p g u c", g=K_PASSES, u=2),
+                in_=grad_wide[i][:].bitcast(F32).rearrange("p (g c u) -> p g u c", g=K_PASSES, u=2),
+            )
+            grad_halves[i] = halves
+
         def turn_grad(i, where=GRAD_BANKS):
-            words = grad_wide[i][:].bitcast(F32)
+            def source(g, u):
+                if i in grad_halves:
+                    return grad_halves[i][:, (2 * g + u) * P : (2 * g + u + 1) * P]
+                return grad_wide[i][:].bitcast(F32)[:, 2 * P * g + u : 2 * P * (g + 1) : 2]
+
             banks = [bank(b) for b in where]
             for g in range(K_PASSES):
                 for u in range(2):
                     at = (2 * (g % 2) + u) * P
                     nc.tensor.transpose(
                         banks[g // 2][:, at : at + P],
-                        words[:, 2 * P * g + u : 2 * P * (g + 1) : 2],
+                        source(g, u),
                         ident_f32[:],
                     )
             grad_banks[i] = banks
@@ -187,24 +200,12 @@ def tile_fp8_gradient_projection_d4_kernel(
                 proj_grouped[g] = work.tile(
                     [P, PACK * R], BF16, name="proj_grouped", tag="proj_grouped", bufs=2, align_bytes=64
                 )
-            dst = proj_grouped[g][:, quarter * 2 * BANK : (quarter + 1) * 2 * BANK]
-            if on_vector:
-                for half in range(2):
-                    nc.vector.tensor_copy(
-                        out=dst[:, half * BANK : (half + 1) * BANK].rearrange("p (c t) -> p c t", t=PACK),
-                        in_=proj_raw[g, 2 * quarter + half].rearrange("p t c -> p c t"),
-                    )
-                return
-            acc = bank(PROJ_BANKS[quarter], BF16)
-            for half in range(2):
-                nc.tensor.matmul(
-                    acc[:, half * BANK : (half + 1) * BANK],
-                    lhsT=ident_bf[:],
-                    rhs=proj_raw[g, 2 * quarter + half].rearrange("p t c -> p c t"),
-                    start=True,
-                    stop=True,
-                )
-            nc.scalar.copy(out=dst, in_=acc[:])
+            dst = proj_grouped[g][:, quarter * PACK * QUARTER : (quarter + 1) * PACK * QUARTER]
+            copy = nc.vector.tensor_copy if on_vector else nc.scalar.copy
+            copy(
+                out=dst.rearrange("p (c i t) -> p c t i", i=4, t=PACK),
+                in_=proj_raw[g, quarter].rearrange("p t (c i) -> p c t i", i=4),
+            )
 
         def quantize_proj(g, first, count):
             cols = slice(first * 2 * P, (first + count) * 2 * P)
@@ -240,7 +241,7 @@ def tile_fp8_gradient_projection_d4_kernel(
 
         def precondition(i, h, engine):
             if h == 0:
-                step[i] = work.tile([P, R], BF16, name="step", tag="step", align_bytes=64)
+                step[i] = work.tile([P, R], BF16, name="step", tag="step", bufs=2, align_bytes=64)
             cols = slice(h * BANK, (h + 1) * BANK)
             engine.tensor_tensor(
                 out=step[i][:, cols].rearrange("p (u c e) -> p u c e", u=2, e=2),
@@ -309,62 +310,62 @@ def tile_fp8_gradient_projection_d4_kernel(
         widen(0, True)
         turn_grad(0)
         empty_grad(0)
+        interleave_proj(0, 0, True)
+        interleave_proj(0, 1)
         widen(1, True)
         turn_grad(1, LOW_BANKS)
-        widen(2, True)
-        interleave_proj(0, 0)
-        empty_grad(1)
-        interleave_proj(0, 1)
-        interleave_proj(0, 2)
-        turn_grad(2)
         quantize_grad(0)
-        interleave_proj(0, 3, True)
+        interleave_proj(0, 2, True)
+        interleave_proj(0, 3)
+        empty_grad(1)
         quantize_proj(0, 0, 2)
-        quantize_grad(1)
-        quantize_proj(0, 2, 2)
-        interleave_proj(1, 0)
+        interleave_proj(1, 0, True)
         interleave_proj(1, 1)
-        interleave_proj(1, 2)
-        empty_grad(2)
-        interleave_proj(1, 3, True)
+        quantize_proj(0, 2, 2)
+        interleave_proj(1, 2, True)
+        interleave_proj(1, 3)
+        quantize_grad(1)
         quantize_proj(1, 0, 2)
-        quantize_proj(1, 2, 2)
         low_banks[0] = [bank(b) for b in LOW_BANKS]
         low_pass(0, 0, 0)
         low_pass(0, 1, 0)
-        interleave_proj(2, 0)
-        interleave_proj(2, 1)
-        interleave_proj(2, 2)
         low_pass(0, 0, 1)
+        interleave_proj(2, 0, True)
+        interleave_proj(2, 1)
+        quantize_proj(1, 2, 2)
         low_pass(0, 1, 1)
-        interleave_proj(2, 3, True)
+        interleave_proj(2, 2, True)
+        interleave_proj(2, 3)
         quantize_proj(2, 0, 2)
-        quantize_proj(2, 2, 1)
-        quantize_proj(2, 3, 1)
         low_pass(0, 0, 2)
+        quantize_proj(2, 2, 2)
         low_pass(0, 1, 2)
-        widen(3)
+        widen(2)
         multiply_low(1, UPD_BANKS[0:2])
+        turn_grad(2)
+        widen(3)
+        empty_grad(2)
         add_mom(0, 0)
         add_mom(0, 1)
         precondition(0, 0, nc.vector)
-        quantize_grad(2)
+        nc.vector.tensor_scalar(out=neg_eta[:], in0=eta_sb[:], scalar1=-1.0, scalar2=None, op0=ALU.mult)
         precondition(0, 1, nc.vector)
-        widen(4)
         turn_grad(3)
-        empty_grad(3)
         add_mom(1, 0)
         add_mom(1, 1)
-        nc.vector.tensor_scalar(out=neg_eta[:], in0=eta_sb[:], scalar1=-1.0, scalar2=None, op0=ALU.mult)
+        empty_grad(3)
         precondition(1, 0, nc.vector)
+        quantize_grad(2)
         precondition(1, 1, nc.vector)
+        widen(4, True)
+        widen(5)
 
         for s in range(2, TILES):
             if s % PAIR == 0 and s >= 4:
-                if s + 2 < TILES:
-                    load_mom_pre(s + 2, PAIR)
                 if s + 4 < TILES:
                     load_grad(s + 4, PAIR)
+                if s + 2 < TILES:
+                    load_mom_pre(s + 2, PAIR)
                 load_w(s, PAIR)
             if s + 2 < TILES:
                 turn_grad(s + 2)
@@ -373,7 +374,9 @@ def tile_fp8_gradient_projection_d4_kernel(
             if s + 2 < TILES:
                 empty_grad(s + 2)
             if s + 3 < TILES:
-                widen(s + 3)
+                split_words(s + 3)
+            if s + 4 < TILES:
+                widen(s + 4)
             if s >= 3:
                 update(s - 3, 2)
             if s + 1 < TILES:

@@ -4,7 +4,7 @@ import concourse.mybir as mybir
 from concourse.masks import make_identity
 
 M, K, R = 1536, 1536, 1024
-FLOPS = 2 * M * K * R * 2
+FLOPS = 2 * M * K * R + 2 * M * R * K
 
 F32 = mybir.dt.float32
 BF16 = mybir.dt.bfloat16
@@ -19,16 +19,17 @@ COPY = mybir.ActivationFunctionType.Copy
 
 P = 128
 PACK = 4
-PASS = P * PACK
 BANK = 512
 TILES = M // P
-K_PASSES = K // PASS
-R_PASSES = R // PASS
-K_BLOCKS = K // P
+K_PASSES = K // (P * PACK)
+R_PASSES = R // (P * PACK)
 K_BANKS = K // BANK
-PAIR = 2
+SCALE_COLS = 128
+SCALES = K // SCALE_COLS
 QUARTER = R // 4
-WARM = 16
+QUADRANT = 32
+PAIR = 2
+BANKWISE_STORES = 4
 
 GRAD_BANKS = (0, 1)
 STEP_BANK = 2
@@ -53,14 +54,13 @@ def tile_fp8_gradient_projection_d4_kernel(
         psum = ctx.enter_context(tc.psum_pool(name="psum", bufs=1))
         ctx.enter_context(tc.manual_schedule())
 
-        def bank(index, dtype=F32):
-            width = BANK if dtype == F32 else 2 * BANK
-            return psum.tile([P, width], dtype, name="bank%d" % index, tag="bank%d" % index)
+        def bank(index):
+            return psum.tile([P, BANK], F32, name="bank%d" % index, tag="bank%d" % index)
 
-        grad_raw, mom_sb, pre_sb, w_sb, proj_raw = {}, {}, {}, {}, {}
-        grad_wide, grad_banks, grad_grouped, grad_q = {}, {}, {}, {}
-        low_banks, total, step, step_bank, step_grouped, step_q = {}, {}, {}, {}, {}, {}
-        upd_banks, proj_grouped, result, grad_halves = {}, {}, {}, {}
+        grad_raw, mom_sb, pre_sb, w_sb, proj_raw, proj_grouped = {}, {}, {}, {}, {}, {}
+        grad_wide, grad_split, grad_turned, grad_grouped, grad_q = {}, {}, {}, {}, {}
+        low, total, step, step_turned, step_grouped, step_q = {}, {}, {}, {}, {}, {}
+        upd, result = {}, {}
 
         def load_rows(store, rows, first, count, width, dtype, label):
             sb = keep.tile([P, count, width], dtype, name="%s%d" % (label, first), align_bytes=64)
@@ -78,7 +78,7 @@ def tile_fp8_gradient_projection_d4_kernel(
         def load_w(first, count):
             load_rows(w_sb, w_rows, first, count, K, BF16, "w_sb")
 
-        def load_proj(g, pieces=1):
+        def load_proj(g, pieces):
             width = R // pieces
             for n in range(pieces):
                 raw = keep.tile([P, PACK, width], BF16, name="proj_raw%d_%d" % (g, n), align_bytes=64)
@@ -86,54 +86,54 @@ def tile_fp8_gradient_projection_d4_kernel(
                 for c in range(width // QUARTER):
                     proj_raw[g, n * width // QUARTER + c] = raw[:, :, c * QUARTER : (c + 1) * QUARTER]
 
-        scale_sb = keep.tile([P, TILES * K_BLOCKS], F32, name="scale_sb")
+        scale_sb = keep.tile([P, TILES * SCALES], F32, name="scale_sb")
         nc.sync.dma_start(out=scale_sb[:], in_=grad_scale.rearrange("(p i) j -> p (i j)", i=TILES))
-        load_grad(0, 1)
-        load_proj(0, 2)
-        load_grad(1, 1)
-        load_proj(1)
-        load_proj(2)
-        load_grad(2, 2)
-        eta_sb = keep.tile([P, TILES], BF16, name="eta_sb")
-        nc.sync.dma_start(out=eta_sb[:], in_=eta.rearrange("(p i) -> p i", i=TILES))
-        load_mom_pre(0, 1)
-        load_mom_pre(1, 1)
-        load_grad(4, 2)
-        load_mom_pre(2, 1)
-
         ident_bf = keep.tile([P, P], BF16, name="ident_bf", align_bytes=64)
         make_identity(nc, ident_bf[:])
         ident_f32 = keep.tile([P, P], F32, name="ident_f32", align_bytes=64)
-        make_identity(nc, ident_f32[:])
+        nc.scalar.activation(out=ident_f32[:], in_=ident_bf[:], func=COPY)
         back_sc = keep.tile([P, R_PASSES, K], U8, name="back_sc", align_bytes=64)
         nc.gpsimd.memset(back_sc[:].rearrange("p g n -> p (g n)").bitcast(I32), 0)
-        table_warm = keep.tile([P, 1], F32, name="table_warm")
-        nc.scalar.activation(out=table_warm[:], in_=ident_f32[:, 0:1], func=COPY, scale=ident_f32[:, 1:2])
-
         back_codes = keep.tile([P, R_PASSES, 2 * K], U8, name="back_codes", align_bytes=64)
-        nc.sync.dma_start(
-            out=back_codes[:].bitcast(I32), in_=back_words.rearrange("g p n -> p g n").bitcast(I32)
-        )
-        for q in range(4):
-            nc.sync.dma_start(
-                out=back_sc[32 * q : 32 * q + 4, :, :].bitcast(I32),
-                in_=back_scales[:, 4 * q : 4 * q + 4, :].rearrange("g q n -> q g n").bitcast(I32),
-            )
-        load_w(0, 1)
-        load_mom_pre(3, 1)
-        load_grad(6, 2)
-        load_w(1, 1)
-        load_mom_pre(4, 2)
-        load_w(2, 2)
-
+        eta_sb = keep.tile([P, TILES], BF16, name="eta_sb")
+        neg_eta = keep.tile([P, TILES], F32, name="neg_eta")
         proj_codes = keep.tile([P, K_PASSES, R], U32, name="proj_codes", align_bytes=64)
         proj_scales = keep.tile([P, K_PASSES, R], U8, name="proj_scales", align_bytes=64)
 
+        def load_back():
+            for q in range(P // QUADRANT):
+                nc.sync.dma_start(
+                    out=back_sc[QUADRANT * q : QUADRANT * q + 4, :, :].bitcast(I32),
+                    in_=back_scales[:, 4 * q : 4 * q + 4, :].rearrange("g q n -> q g n").bitcast(I32),
+                )
+            nc.sync.dma_start(
+                out=back_codes[:].bitcast(I32), in_=back_words.rearrange("g p n -> p g n").bitcast(I32)
+            )
+
+        def interleave_proj(g, quarter, copy):
+            if g not in proj_grouped:
+                proj_grouped[g] = work.tile(
+                    [P, PACK * R], BF16, name="proj_grouped", tag="proj_grouped", bufs=2, align_bytes=64
+                )
+            dst = proj_grouped[g][:, quarter * PACK * QUARTER : (quarter + 1) * PACK * QUARTER]
+            copy(
+                out=dst.rearrange("p (c i t) -> p c t i", i=4, t=PACK),
+                in_=proj_raw[g, quarter].rearrange("p t (c i) -> p c t i", i=4),
+            )
+
+        def quantize_proj(g, h):
+            cols = slice(h * BANK, (h + 1) * BANK)
+            nc.vector.quantize_mx(
+                out=proj_codes[:, g, cols].bitcast(FP8X4),
+                scales=proj_scales[:, g, cols],
+                in_=proj_grouped[g][:, PACK * cols.start : PACK * cols.stop],
+            )
+
         def widen(i, on_vector=False):
             wide = work.tile([P, K], BF16, name="grad_wide", tag="grad_wide", align_bytes=64)
-            for j in range(K_BLOCKS):
-                cols = slice(j * P, (j + 1) * P)
-                factor = scale_sb[:, i * K_BLOCKS + j : i * K_BLOCKS + j + 1]
+            for j in range(SCALES):
+                cols = slice(j * SCALE_COLS, (j + 1) * SCALE_COLS)
+                factor = scale_sb[:, i * SCALES + j : i * SCALES + j + 1]
                 src = grad_raw[i][:, cols].bitcast(FP8)
                 if on_vector:
                     nc.vector.tensor_scalar(
@@ -143,42 +143,35 @@ def tile_fp8_gradient_projection_d4_kernel(
                     nc.scalar.activation(out=wide[:, cols], in_=src, func=COPY, scale=factor)
             grad_wide[i] = wide
 
-        def split_words(i, on_vector=False):
-            halves = work.tile([P, K // 2], F32, name="grad_halves", tag="grad_halves", bufs=2, align_bytes=64)
-            copy = nc.vector.tensor_copy if on_vector else nc.scalar.copy
-            copy(
-                out=halves[:].rearrange("p (g u c) -> p g u c", g=K_PASSES, u=2),
+        def split_words(i):
+            split = work.tile([P, K // 2], F32, name="grad_split", tag="grad_split", bufs=2, align_bytes=64)
+            nc.scalar.copy(
+                out=split[:].rearrange("p (g u c) -> p g u c", g=K_PASSES, u=2),
                 in_=grad_wide[i][:].bitcast(F32).rearrange("p (g c u) -> p g u c", g=K_PASSES, u=2),
             )
-            grad_halves[i] = halves
+            grad_split[i] = split
 
         def turn_grad(i, where=GRAD_BANKS):
-            def source(g, u):
-                if i in grad_halves:
-                    return grad_halves[i][:, (2 * g + u) * P : (2 * g + u + 1) * P]
-                return grad_wide[i][:].bitcast(F32)[:, 2 * P * g + u : 2 * P * (g + 1) : 2]
-
             banks = [bank(b) for b in where]
             for g in range(K_PASSES):
                 for u in range(2):
+                    if i in grad_split:
+                        words = grad_split[i][:, (2 * g + u) * P : (2 * g + u + 1) * P]
+                    else:
+                        words = grad_wide[i][:].bitcast(F32)[:, 2 * P * g + u : 2 * P * (g + 1) : 2]
                     at = (2 * (g % 2) + u) * P
-                    nc.tensor.transpose(
-                        banks[g // 2][:, at : at + P],
-                        source(g, u),
-                        ident_f32[:],
-                    )
-            grad_banks[i] = banks
+                    nc.tensor.transpose(banks[g // 2][:, at : at + P], words, ident_f32[:])
+            grad_turned[i] = banks
 
-        def empty_grad(i, on_vector=False):
-            copy = nc.vector.tensor_copy if on_vector else nc.scalar.copy
+        def empty_grad(i):
             grouped = work.tile([P, K], BF16, name="grad_grouped", tag="grad_grouped", align_bytes=64)
             words = grouped[:].bitcast(F32)
-            first, second = grad_banks[i]
-            copy(
+            first, second = grad_turned[i]
+            nc.scalar.copy(
                 out=words[:, 0 : 4 * P].rearrange("p (g m u) -> p g m u", g=2, u=2),
                 in_=first[:].rearrange("p (g u m) -> p g m u", g=2, u=2),
             )
-            copy(
+            nc.scalar.copy(
                 out=words[:, 4 * P : 6 * P].rearrange("p (m u) -> p m u", u=2),
                 in_=second[:, 0 : 2 * P].rearrange("p (u m) -> p m u", u=2),
             )
@@ -195,30 +188,12 @@ def tile_fp8_gradient_projection_d4_kernel(
                 )
             grad_q[i] = (codes, scales)
 
-        def interleave_proj(g, quarter, on_vector=False):
-            if quarter == 0:
-                proj_grouped[g] = work.tile(
-                    [P, PACK * R], BF16, name="proj_grouped", tag="proj_grouped", bufs=2, align_bytes=64
-                )
-            dst = proj_grouped[g][:, quarter * PACK * QUARTER : (quarter + 1) * PACK * QUARTER]
-            copy = nc.vector.tensor_copy if on_vector else nc.scalar.copy
-            copy(
-                out=dst.rearrange("p (c i t) -> p c t i", i=4, t=PACK),
-                in_=proj_raw[g, quarter].rearrange("p t (c i) -> p c t i", i=4),
-            )
-
-        def quantize_proj(g, first, count):
-            cols = slice(first * 2 * P, (first + count) * 2 * P)
-            nc.vector.quantize_mx(
-                out=proj_codes[:, g, cols].bitcast(FP8X4),
-                scales=proj_scales[:, g, cols],
-                in_=proj_grouped[g][:, PACK * cols.start : PACK * cols.stop],
-            )
-
-        def low_pass(i, h, g):
+        def low_pass(i, h, g, where):
             codes, scales = grad_q[i]
+            if g == 0:
+                low[i, h] = bank(where)
             nc.tensor.matmul_mx(
-                out=low_banks[i][h][:],
+                out=low[i, h][:],
                 lhsT=codes[:, g * P : (g + 1) * P].bitcast(FP8X4),
                 lhsT_scale=scales[:, g * P : (g + 1) * P],
                 rhs=proj_codes[:, g, h * BANK : (h + 1) * BANK].bitcast(FP8X4),
@@ -227,20 +202,19 @@ def tile_fp8_gradient_projection_d4_kernel(
                 stop=(g == K_PASSES - 1),
             )
 
-        def multiply_low(i, banks=LOW_BANKS):
-            low_banks[i] = [bank(b) for b in banks]
+        def multiply_low(i, where=LOW_BANKS):
             for h in range(R_PASSES):
                 for g in range(K_PASSES):
-                    low_pass(i, h, g)
+                    low_pass(i, h, g, where[h])
 
         def add_mom(i, h):
-            if h == 0:
+            if i not in total:
                 total[i] = work.tile([P, R], F32, name="total", tag="total", bufs=2, align_bytes=64)
             cols = slice(h * BANK, (h + 1) * BANK)
-            nc.vector.tensor_tensor(out=total[i][:, cols], in0=low_banks[i][h][:], in1=mom_sb[i][:, cols], op=ALU.add)
+            nc.vector.tensor_tensor(out=total[i][:, cols], in0=low[i, h][:], in1=mom_sb[i][:, cols], op=ALU.add)
 
         def precondition(i, h, engine):
-            if h == 0:
+            if i not in step:
                 step[i] = work.tile([P, R], BF16, name="step", tag="step", bufs=2, align_bytes=64)
             cols = slice(h * BANK, (h + 1) * BANK)
             engine.tensor_tensor(
@@ -252,16 +226,16 @@ def tile_fp8_gradient_projection_d4_kernel(
 
         def turn_step(i, where=STEP_BANK):
             words = step[i][:].bitcast(F32)
-            acc = bank(where)
-            for n in range(4):
-                nc.tensor.transpose(acc[:, n * P : (n + 1) * P], words[:, n * P : (n + 1) * P], ident_f32[:])
-            step_bank[i] = acc
+            turned = bank(where)
+            for n in range(2 * R_PASSES):
+                nc.tensor.transpose(turned[:, n * P : (n + 1) * P], words[:, n * P : (n + 1) * P], ident_f32[:])
+            step_turned[i] = turned
 
         def empty_step(i):
             grouped = work.tile([P, R], BF16, name="step_grouped", tag="step_grouped", bufs=2, align_bytes=64)
             nc.scalar.copy(
-                out=grouped[:].bitcast(F32).rearrange("p (h m u) -> p h m u", h=2, u=2),
-                in_=step_bank[i][:].rearrange("p (h u m) -> p h m u", h=2, u=2),
+                out=grouped[:].bitcast(F32).rearrange("p (h m u) -> p h m u", m=P, u=2),
+                in_=step_turned[i][:].rearrange("p (h u m) -> p h m u", m=P, u=2),
             )
             step_grouped[i] = grouped
 
@@ -271,138 +245,200 @@ def tile_fp8_gradient_projection_d4_kernel(
             nc.vector.quantize_mx(out=codes[:].bitcast(FP8X4), scales=scales[:], in_=step_grouped[i][:])
             step_q[i] = (codes, scales)
 
-        def multiply_upd(i, banks=UPD_BANKS):
+        def multiply_upd(i, n, where):
             codes, scales = step_q[i]
-            upd_banks[i] = [bank(b) for b in banks]
+            upd[i, n] = bank(where)
+            for h in range(R_PASSES):
+                nc.tensor.matmul_mx(
+                    out=upd[i, n][:],
+                    lhsT=codes[:, h * P : (h + 1) * P].bitcast(FP8X4),
+                    lhsT_scale=scales[:, h * P : (h + 1) * P],
+                    rhs=back_codes[:, h, 2 * n * BANK : 2 * (n + 1) * BANK].bitcast(FP4X4),
+                    rhs_scale=back_sc[:, h, n * BANK : (n + 1) * BANK],
+                    start=(h == 0),
+                    stop=(h == R_PASSES - 1),
+                )
+
+        def multiply_upd_tile(i, where=UPD_BANKS):
             for n in range(K_BANKS):
-                for h in range(R_PASSES):
-                    nc.tensor.matmul_mx(
-                        out=upd_banks[i][n][:],
-                        lhsT=codes[:, h * P : (h + 1) * P].bitcast(FP8X4),
-                        lhsT_scale=scales[:, h * P : (h + 1) * P],
-                        rhs=back_codes[:, h, 2 * n * BANK : 2 * (n + 1) * BANK].bitcast(FP4X4),
-                        rhs_scale=back_sc[:, h, n * BANK : (n + 1) * BANK],
-                        start=(h == 0),
-                        stop=(h == R_PASSES - 1),
-                    )
+                multiply_upd(i, n, where[n])
 
         def update(i, n):
             if n == 0:
-                result[i] = work.tile([P, K], F32, name="result", tag="result", bufs=3, align_bytes=64)
+                result[i] = work.tile([P, K], F32, name="result", tag="result", align_bytes=64)
             cols = slice(n * BANK, (n + 1) * BANK)
             nc.vector.scalar_tensor_tensor(
                 out=result[i][:, cols],
-                in0=upd_banks[i][n][:],
+                in0=upd[i, n][:],
                 scalar=neg_eta[:, i : i + 1],
                 in1=w_sb[i][:, cols],
                 op0=ALU.mult,
                 op1=ALU.add,
             )
-            if i >= TILES - 2:
+            if i >= TILES - BANKWISE_STORES:
                 nc.sync.dma_start(out=out_rows[:, i, cols], in_=result[i][:, cols])
             elif n == K_BANKS - 1:
                 nc.sync.dma_start(out=out_rows[:, i, :], in_=result[i][:])
 
-        warm = bank(LOW_BANKS[0])
-        for n in range(WARM):
-            nc.tensor.matmul(warm[:, 0:P], lhsT=ident_bf[:], rhs=ident_bf[:], start=True, stop=True)
-        neg_eta = keep.tile([P, TILES], F32, name="neg_eta")
-        widen(0, True)
+        on_vector, on_scalar = nc.vector.tensor_copy, nc.scalar.copy
+
+        load_grad(0, 1)
+        load_grad(1, 1)
+        load_proj(0, 2)
+        load_grad(2, 1)
+        load_proj(1, 1)
+        load_proj(2, 1)
+        load_mom_pre(0, 1)
+        nc.sync.dma_start(out=eta_sb[:], in_=eta.rearrange("(p i) -> p i", i=TILES))
+        load_grad(3, 1)
+        load_mom_pre(1, 1)
+        load_grad(4, PAIR)
+        load_back()
+        load_mom_pre(2, 1)
+        load_w(0, 1)
+        load_grad(6, PAIR)
+        load_mom_pre(3, 1)
+        load_w(1, 1)
+        load_mom_pre(4, PAIR)
+        load_w(2, PAIR)
+
+        def first_low_passes(h, g):
+            low_pass(0, h, g, LOW_BANKS[h])
+            low_pass(1, h, g, UPD_BANKS[h])
+
+        widen(0)
+        widen(1, on_vector=True)
         turn_grad(0)
+        turn_grad(1, (UPD_BANKS[2], STEP_BANK))
+        interleave_proj(0, 0, on_scalar)
         empty_grad(0)
-        interleave_proj(0, 0, True)
-        interleave_proj(0, 1)
-        widen(1, True)
-        turn_grad(1, LOW_BANKS)
-        quantize_grad(0)
-        interleave_proj(0, 2, True)
-        interleave_proj(0, 3)
-        empty_grad(1)
-        quantize_proj(0, 0, 2)
-        interleave_proj(1, 0, True)
-        interleave_proj(1, 1)
-        quantize_proj(0, 2, 2)
-        interleave_proj(1, 2, True)
-        interleave_proj(1, 3)
-        quantize_grad(1)
-        quantize_proj(1, 0, 2)
-        low_banks[0] = [bank(b) for b in LOW_BANKS]
-        low_pass(0, 0, 0)
-        low_pass(0, 1, 0)
-        low_pass(0, 0, 1)
-        interleave_proj(2, 0, True)
-        interleave_proj(2, 1)
-        quantize_proj(1, 2, 2)
-        low_pass(0, 1, 1)
-        interleave_proj(2, 2, True)
-        interleave_proj(2, 3)
-        quantize_proj(2, 0, 2)
-        low_pass(0, 0, 2)
-        quantize_proj(2, 2, 2)
-        low_pass(0, 1, 2)
         widen(2)
-        multiply_low(1, UPD_BANKS[0:2])
+        empty_grad(1)
         turn_grad(2)
-        widen(3)
+        for quarter in (1, 2, 3):
+            interleave_proj(0, quarter, on_vector)
+        quantize_proj(0, 0)
+        quantize_grad(0)
+        quantize_proj(0, 1)
+
+        for quarter in (2, 3):
+            interleave_proj(1, quarter, on_scalar)
+        for quarter in (0, 1):
+            interleave_proj(1, quarter, on_vector)
+        quantize_grad(1)
+        first_low_passes(0, 0)
+        first_low_passes(1, 0)
+        quantize_proj(1, 0)
+        first_low_passes(0, 1)
+
+        interleave_proj(2, 3, on_scalar)
+        for quarter in (0, 1):
+            interleave_proj(2, quarter, on_vector)
+        quantize_proj(1, 1)
+        interleave_proj(2, 2, on_vector)
+        first_low_passes(1, 1)
+        quantize_proj(2, 0)
+        first_low_passes(0, 2)
         empty_grad(2)
+        widen(3)
+        widen(4)
+        quantize_proj(2, 1)
+        first_low_passes(1, 2)
+
         add_mom(0, 0)
-        add_mom(0, 1)
-        precondition(0, 0, nc.vector)
-        nc.vector.tensor_scalar(out=neg_eta[:], in0=eta_sb[:], scalar1=-1.0, scalar2=None, op0=ALU.mult)
-        precondition(0, 1, nc.vector)
-        turn_grad(3)
+        precondition(0, 0, nc.gpsimd)
         add_mom(1, 0)
+        add_mom(0, 1)
         add_mom(1, 1)
+        precondition(0, 1, nc.vector)
+        quantize_grad(2)
+        turn_grad(3)
         empty_grad(3)
         precondition(1, 0, nc.vector)
-        quantize_grad(2)
+        nc.vector.tensor_scalar(out=neg_eta[:], in0=eta_sb[:], scalar1=-1.0, scalar2=None, op0=ALU.mult)
         precondition(1, 1, nc.vector)
-        widen(4, True)
-        widen(5)
 
-        for s in range(2, TILES):
-            if s % PAIR == 0 and s >= 4:
+        def finish_round(s):
+            add_mom(s, 0)
+            precondition(s, 0, nc.gpsimd)
+            add_mom(s, 1)
+            multiply_upd_tile(s - 2)
+            update(s - 2, 0)
+            update(s - 2, 1)
+            precondition(s, 1, nc.vector)
+
+        first = 2
+        turn_step(first - 2)
+        empty_step(first - 2)
+        widen(first + 3)
+        quantize_grad(first + 1)
+        quantize_step(first - 2)
+        multiply_low(first)
+        turn_grad(first + 2)
+        empty_grad(first + 2)
+        widen(first + 4)
+        finish_round(first)
+
+        for s in range(first + 1, TILES - 2):
+            if s % PAIR == 0:
                 if s + 4 < TILES:
                     load_grad(s + 4, PAIR)
-                if s + 2 < TILES:
-                    load_mom_pre(s + 2, PAIR)
+                load_mom_pre(s + 2, PAIR)
                 load_w(s, PAIR)
-            if s + 2 < TILES:
-                turn_grad(s + 2)
+            turn_grad(s + 2)
             turn_step(s - 2)
             empty_step(s - 2)
-            if s + 2 < TILES:
-                empty_grad(s + 2)
+            empty_grad(s + 2)
             if s + 3 < TILES:
                 split_words(s + 3)
             if s + 4 < TILES:
                 widen(s + 4)
-            if s >= 3:
-                update(s - 3, 2)
-            if s + 1 < TILES:
-                quantize_grad(s + 1)
+            update(s - 3, 2)
+            quantize_grad(s + 1)
             quantize_step(s - 2)
             multiply_low(s)
-            add_mom(s, 0)
-            precondition(s, 0, nc.gpsimd)
-            add_mom(s, 1)
-            precondition(s, 1, nc.gpsimd)
-            if s == TILES - 1:
-                turn_step(s - 1)
-                empty_step(s - 1)
-            multiply_upd(s - 2)
-            update(s - 2, 0)
-            update(s - 2, 1)
-        update(TILES - 3, 2)
-        quantize_step(TILES - 2)
-        turn_step(TILES - 1)
-        empty_step(TILES - 1)
-        multiply_upd(TILES - 2, LOW_BANKS + GRAD_BANKS[0:1])
-        update(TILES - 2, 0)
-        quantize_step(TILES - 1)
-        multiply_upd(TILES - 1)
-        update(TILES - 2, 1)
-        update(TILES - 2, 2)
-        update(TILES - 1, 0)
-        update(TILES - 1, 1)
-        update(TILES - 1, 2)
+            finish_round(s)
+
+        a, b, c, d = range(TILES - 4, TILES)
+        load_w(c, PAIR)
+        turn_step(a, 2)
+        turn_step(b, 0)
+        empty_step(a)
+        empty_step(b)
+        quantize_grad(d)
+        quantize_step(a)
+        update(a - 1, 2)
+        multiply_low(c, (3, 4))
+        add_mom(c, 0)
+        precondition(c, 0, nc.gpsimd)
+        add_mom(c, 1)
+        multiply_upd(a, 0, 5)
+        multiply_upd(a, 1, 6)
+        multiply_low(d, (1, 2))
+        update(a, 0)
+        update(a, 1)
+        quantize_step(b)
+        add_mom(d, 0)
+        precondition(c, 1, nc.vector)
+        precondition(d, 0, nc.gpsimd)
+        multiply_upd(a, 2, 7)
+        add_mom(d, 1)
+        update(a, 2)
+        multiply_upd(b, 0, 3)
+        turn_step(c, 0)
+        empty_step(c)
+        update(b, 0)
+        precondition(d, 1, nc.vector)
+        multiply_upd(b, 1, 4)
+        multiply_upd(b, 2, 5)
+        turn_step(d, 6)
+        empty_step(d)
+        quantize_step(c)
+        multiply_upd_tile(c, (1, 2, 7))
+        update(b, 1)
+        update(b, 2)
+        quantize_step(d)
+        multiply_upd_tile(d, (0, 3, 4))
+        for i in (c, d):
+            for n in range(K_BANKS):
+                update(i, n)

from contextlib import ExitStack

import concourse.mybir as mybir
from concourse.masks import make_identity

M, K, R = 1536, 1536, 1024
FLOPS = 2 * M * K * R + 2 * M * R * K

F32 = mybir.dt.float32
BF16 = mybir.dt.bfloat16
I32 = mybir.dt.int32
U32 = mybir.dt.uint32
U8 = mybir.dt.uint8
FP8 = mybir.dt.float8_e4m3fn
FP8X4 = mybir.dt.float8_e4m3fn_x4
FP4X4 = mybir.dt.float4_e2m1fn_x4
ALU = mybir.AluOpType
COPY = mybir.ActivationFunctionType.Copy

P = 128
PACK = 4
BANK = 512
TILES = M // P
K_PASSES = K // (P * PACK)
R_PASSES = R // (P * PACK)
K_BANKS = K // BANK
SCALE_COLS = 128
SCALES = K // SCALE_COLS
QUARTER = R // 4
QUADRANT = 32
PAIR = 2
BANKWISE_STORES = 4

GRAD_BANKS = (0, 1)
STEP_BANK = 2
LOW_BANKS = (3, 4)
UPD_BANKS = (5, 6, 7)


def tile_fp8_gradient_projection_d4_kernel(
    tc, grad_bytes, grad_scale, proj, mom, pre, back_words, back_scales, w, eta, out
):
    nc = tc.nc
    grad_rows = grad_bytes.rearrange("(p i) k -> p i k", i=TILES)
    mom_rows = mom.rearrange("(p i) r -> p i r", i=TILES)
    pre_rows = pre.rearrange("(p i) r -> p i r", i=TILES)
    w_rows = w.rearrange("(p i) k -> p i k", i=TILES)
    out_rows = out.rearrange("(p i) k -> p i k", i=TILES)
    proj_rows = proj.rearrange("(g p t) r -> g p t r", p=P, t=PACK)

    with ExitStack() as ctx:
        keep = ctx.enter_context(tc.tile_pool(name="keep", bufs=1))
        work = ctx.enter_context(tc.tile_pool(name="work", bufs=3))
        psum = ctx.enter_context(tc.psum_pool(name="psum", bufs=1))
        ctx.enter_context(tc.manual_schedule())

        def bank(index):
            return psum.tile([P, BANK], F32, name="bank%d" % index, tag="bank%d" % index)

        grad_raw, mom_sb, pre_sb, w_sb, proj_raw, proj_grouped = {}, {}, {}, {}, {}, {}
        grad_wide, grad_split, grad_turned, grad_grouped, grad_q = {}, {}, {}, {}, {}
        low, total, step, step_turned, step_grouped, step_q = {}, {}, {}, {}, {}, {}
        upd, result = {}, {}

        def load_rows(store, rows, first, count, width, dtype, label):
            sb = keep.tile([P, count, width], dtype, name="%s%d" % (label, first), align_bytes=64)
            nc.sync.dma_start(out=sb[:], in_=rows[:, first : first + count, :])
            for j in range(count):
                store[first + j] = sb[:, j, :]

        def load_grad(first, count):
            load_rows(grad_raw, grad_rows, first, count, K, U8, "grad_raw")

        def load_mom_pre(first, count):
            load_rows(mom_sb, mom_rows, first, count, R, BF16, "mom_sb")
            load_rows(pre_sb, pre_rows, first, count, R, BF16, "pre_sb")

        def load_w(first, count):
            load_rows(w_sb, w_rows, first, count, K, BF16, "w_sb")

        def load_proj(g, pieces):
            width = R // pieces
            for n in range(pieces):
                raw = keep.tile([P, PACK, width], BF16, name="proj_raw%d_%d" % (g, n), align_bytes=64)
                nc.sync.dma_start(out=raw[:], in_=proj_rows[g][:, :, n * width : (n + 1) * width])
                for c in range(width // QUARTER):
                    proj_raw[g, n * width // QUARTER + c] = raw[:, :, c * QUARTER : (c + 1) * QUARTER]

        scale_sb = keep.tile([P, TILES * SCALES], F32, name="scale_sb")
        nc.sync.dma_start(out=scale_sb[:], in_=grad_scale.rearrange("(p i) j -> p (i j)", i=TILES))
        ident_bf = keep.tile([P, P], BF16, name="ident_bf", align_bytes=64)
        make_identity(nc, ident_bf[:])
        ident_f32 = keep.tile([P, P], F32, name="ident_f32", align_bytes=64)
        nc.scalar.activation(out=ident_f32[:], in_=ident_bf[:], func=COPY)
        back_sc = keep.tile([P, R_PASSES, K], U8, name="back_sc", align_bytes=64)
        nc.gpsimd.memset(back_sc[:].rearrange("p g n -> p (g n)").bitcast(I32), 0)
        back_codes = keep.tile([P, R_PASSES, 2 * K], U8, name="back_codes", align_bytes=64)
        eta_sb = keep.tile([P, TILES], BF16, name="eta_sb")
        neg_eta = keep.tile([P, TILES], F32, name="neg_eta")
        proj_codes = keep.tile([P, K_PASSES, R], U32, name="proj_codes", align_bytes=64)
        proj_scales = keep.tile([P, K_PASSES, R], U8, name="proj_scales", align_bytes=64)

        def load_back():
            for q in range(P // QUADRANT):
                nc.sync.dma_start(
                    out=back_sc[QUADRANT * q : QUADRANT * q + 4, :, :].bitcast(I32),
                    in_=back_scales[:, 4 * q : 4 * q + 4, :].rearrange("g q n -> q g n").bitcast(I32),
                )
            nc.sync.dma_start(
                out=back_codes[:].bitcast(I32), in_=back_words.rearrange("g p n -> p g n").bitcast(I32)
            )

        def interleave_proj(g, quarter, copy):
            if g not in proj_grouped:
                proj_grouped[g] = work.tile(
                    [P, PACK * R], BF16, name="proj_grouped", tag="proj_grouped", bufs=2, align_bytes=64
                )
            dst = proj_grouped[g][:, quarter * PACK * QUARTER : (quarter + 1) * PACK * QUARTER]
            copy(
                out=dst.rearrange("p (c i t) -> p c t i", i=4, t=PACK),
                in_=proj_raw[g, quarter].rearrange("p t (c i) -> p c t i", i=4),
            )

        def quantize_proj(g, h):
            cols = slice(h * BANK, (h + 1) * BANK)
            nc.vector.quantize_mx(
                out=proj_codes[:, g, cols].bitcast(FP8X4),
                scales=proj_scales[:, g, cols],
                in_=proj_grouped[g][:, PACK * cols.start : PACK * cols.stop],
            )

        def widen(i, on_vector=False):
            wide = work.tile([P, K], BF16, name="grad_wide", tag="grad_wide", align_bytes=64)
            for j in range(SCALES):
                cols = slice(j * SCALE_COLS, (j + 1) * SCALE_COLS)
                factor = scale_sb[:, i * SCALES + j : i * SCALES + j + 1]
                src = grad_raw[i][:, cols].bitcast(FP8)
                if on_vector:
                    nc.vector.tensor_scalar(
                        out=wide[:, cols], in0=src, scalar1=factor, scalar2=None, op0=ALU.mult
                    )
                else:
                    nc.scalar.activation(out=wide[:, cols], in_=src, func=COPY, scale=factor)
            grad_wide[i] = wide

        def split_words(i):
            split = work.tile([P, K // 2], F32, name="grad_split", tag="grad_split", bufs=2, align_bytes=64)
            nc.scalar.copy(
                out=split[:].rearrange("p (g u c) -> p g u c", g=K_PASSES, u=2),
                in_=grad_wide[i][:].bitcast(F32).rearrange("p (g c u) -> p g u c", g=K_PASSES, u=2),
            )
            grad_split[i] = split

        def turn_grad(i, where=GRAD_BANKS):
            banks = [bank(b) for b in where]
            for g in range(K_PASSES):
                for u in range(2):
                    if i in grad_split:
                        words = grad_split[i][:, (2 * g + u) * P : (2 * g + u + 1) * P]
                    else:
                        words = grad_wide[i][:].bitcast(F32)[:, 2 * P * g + u : 2 * P * (g + 1) : 2]
                    at = (2 * (g % 2) + u) * P
                    nc.tensor.transpose(banks[g // 2][:, at : at + P], words, ident_f32[:])
            grad_turned[i] = banks

        def empty_grad(i):
            grouped = work.tile([P, K], BF16, name="grad_grouped", tag="grad_grouped", align_bytes=64)
            words = grouped[:].bitcast(F32)
            first, second = grad_turned[i]
            nc.scalar.copy(
                out=words[:, 0 : 4 * P].rearrange("p (g m u) -> p g m u", g=2, u=2),
                in_=first[:].rearrange("p (g u m) -> p g m u", g=2, u=2),
            )
            nc.scalar.copy(
                out=words[:, 4 * P : 6 * P].rearrange("p (m u) -> p m u", u=2),
                in_=second[:, 0 : 2 * P].rearrange("p (u m) -> p m u", u=2),
            )
            grad_grouped[i] = grouped

        def quantize_grad(i):
            codes = work.tile([P, K_PASSES * P], U32, name="grad_codes", tag="grad_codes", align_bytes=64)
            scales = work.tile([P, K_PASSES * P], U8, name="grad_scales", tag="grad_scales", align_bytes=64)
            for lo, hi in ((0, 2 * P), (2 * P, 3 * P)):
                nc.vector.quantize_mx(
                    out=codes[:, lo:hi].bitcast(FP8X4),
                    scales=scales[:, lo:hi],
                    in_=grad_grouped[i][:, PACK * lo : PACK * hi],
                )
            grad_q[i] = (codes, scales)

        def low_pass(i, h, g, where):
            codes, scales = grad_q[i]
            if g == 0:
                low[i, h] = bank(where)
            nc.tensor.matmul_mx(
                out=low[i, h][:],
                lhsT=codes[:, g * P : (g + 1) * P].bitcast(FP8X4),
                lhsT_scale=scales[:, g * P : (g + 1) * P],
                rhs=proj_codes[:, g, h * BANK : (h + 1) * BANK].bitcast(FP8X4),
                rhs_scale=proj_scales[:, g, h * BANK : (h + 1) * BANK],
                start=(g == 0),
                stop=(g == K_PASSES - 1),
            )

        def multiply_low(i, where=LOW_BANKS):
            for h in range(R_PASSES):
                for g in range(K_PASSES):
                    low_pass(i, h, g, where[h])

        def add_mom(i, h):
            if i not in total:
                total[i] = work.tile([P, R], F32, name="total", tag="total", bufs=2, align_bytes=64)
            cols = slice(h * BANK, (h + 1) * BANK)
            nc.vector.tensor_tensor(out=total[i][:, cols], in0=low[i, h][:], in1=mom_sb[i][:, cols], op=ALU.add)

        def precondition(i, h, engine):
            if i not in step:
                step[i] = work.tile([P, R], BF16, name="step", tag="step", bufs=2, align_bytes=64)
            cols = slice(h * BANK, (h + 1) * BANK)
            engine.tensor_tensor(
                out=step[i][:, cols].rearrange("p (u c e) -> p u c e", u=2, e=2),
                in0=total[i][:, cols].rearrange("p (c u e) -> p u c e", u=2, e=2),
                in1=pre_sb[i][:, cols].rearrange("p (c u e) -> p u c e", u=2, e=2),
                op=ALU.mult,
            )

        def turn_step(i, where=STEP_BANK):
            words = step[i][:].bitcast(F32)
            turned = bank(where)
            for n in range(2 * R_PASSES):
                nc.tensor.transpose(turned[:, n * P : (n + 1) * P], words[:, n * P : (n + 1) * P], ident_f32[:])
            step_turned[i] = turned

        def empty_step(i):
            grouped = work.tile([P, R], BF16, name="step_grouped", tag="step_grouped", bufs=2, align_bytes=64)
            nc.scalar.copy(
                out=grouped[:].bitcast(F32).rearrange("p (h m u) -> p h m u", m=P, u=2),
                in_=step_turned[i][:].rearrange("p (h u m) -> p h m u", m=P, u=2),
            )
            step_grouped[i] = grouped

        def quantize_step(i):
            codes = work.tile([P, R_PASSES * P], U32, name="step_codes", tag="step_codes", align_bytes=64)
            scales = work.tile([P, R_PASSES * P], U8, name="step_scales", tag="step_scales", align_bytes=64)
            nc.vector.quantize_mx(out=codes[:].bitcast(FP8X4), scales=scales[:], in_=step_grouped[i][:])
            step_q[i] = (codes, scales)

        def multiply_upd(i, n, where):
            codes, scales = step_q[i]
            upd[i, n] = bank(where)
            for h in range(R_PASSES):
                nc.tensor.matmul_mx(
                    out=upd[i, n][:],
                    lhsT=codes[:, h * P : (h + 1) * P].bitcast(FP8X4),
                    lhsT_scale=scales[:, h * P : (h + 1) * P],
                    rhs=back_codes[:, h, 2 * n * BANK : 2 * (n + 1) * BANK].bitcast(FP4X4),
                    rhs_scale=back_sc[:, h, n * BANK : (n + 1) * BANK],
                    start=(h == 0),
                    stop=(h == R_PASSES - 1),
                )

        def multiply_upd_tile(i, where=UPD_BANKS):
            for n in range(K_BANKS):
                multiply_upd(i, n, where[n])

        def update(i, n):
            if n == 0:
                result[i] = work.tile([P, K], F32, name="result", tag="result", align_bytes=64)
            cols = slice(n * BANK, (n + 1) * BANK)
            nc.vector.scalar_tensor_tensor(
                out=result[i][:, cols],
                in0=upd[i, n][:],
                scalar=neg_eta[:, i : i + 1],
                in1=w_sb[i][:, cols],
                op0=ALU.mult,
                op1=ALU.add,
            )
            if i >= TILES - BANKWISE_STORES:
                nc.sync.dma_start(out=out_rows[:, i, cols], in_=result[i][:, cols])
            elif n == K_BANKS - 1:
                nc.sync.dma_start(out=out_rows[:, i, :], in_=result[i][:])

        on_vector, on_scalar = nc.vector.tensor_copy, nc.scalar.copy

        load_grad(0, 1)
        load_grad(1, 1)
        load_proj(0, 2)
        load_grad(2, 1)
        load_proj(1, 1)
        load_proj(2, 1)
        load_mom_pre(0, 1)
        nc.sync.dma_start(out=eta_sb[:], in_=eta.rearrange("(p i) -> p i", i=TILES))
        load_grad(3, 1)
        load_mom_pre(1, 1)
        load_grad(4, PAIR)
        load_back()
        load_mom_pre(2, 1)
        load_w(0, 1)
        load_grad(6, PAIR)
        load_mom_pre(3, 1)
        load_w(1, 1)
        load_mom_pre(4, PAIR)
        load_w(2, PAIR)

        def first_low_passes(h, g):
            low_pass(0, h, g, LOW_BANKS[h])
            low_pass(1, h, g, UPD_BANKS[h])

        widen(0)
        widen(1, on_vector=True)
        turn_grad(0)
        turn_grad(1, (UPD_BANKS[2], STEP_BANK))
        interleave_proj(0, 0, on_scalar)
        empty_grad(0)
        widen(2)
        empty_grad(1)
        turn_grad(2)
        for quarter in (1, 2, 3):
            interleave_proj(0, quarter, on_vector)
        quantize_proj(0, 0)
        quantize_grad(0)
        quantize_proj(0, 1)

        for quarter in (2, 3):
            interleave_proj(1, quarter, on_scalar)
        for quarter in (0, 1):
            interleave_proj(1, quarter, on_vector)
        quantize_grad(1)
        first_low_passes(0, 0)
        first_low_passes(1, 0)
        quantize_proj(1, 0)
        first_low_passes(0, 1)

        interleave_proj(2, 3, on_scalar)
        for quarter in (0, 1):
            interleave_proj(2, quarter, on_vector)
        quantize_proj(1, 1)
        interleave_proj(2, 2, on_vector)
        first_low_passes(1, 1)
        quantize_proj(2, 0)
        first_low_passes(0, 2)
        empty_grad(2)
        widen(3)
        widen(4)
        quantize_proj(2, 1)
        first_low_passes(1, 2)

        add_mom(0, 0)
        precondition(0, 0, nc.gpsimd)
        add_mom(1, 0)
        add_mom(0, 1)
        add_mom(1, 1)
        precondition(0, 1, nc.vector)
        quantize_grad(2)
        turn_grad(3)
        empty_grad(3)
        precondition(1, 0, nc.vector)
        nc.vector.tensor_scalar(out=neg_eta[:], in0=eta_sb[:], scalar1=-1.0, scalar2=None, op0=ALU.mult)
        precondition(1, 1, nc.vector)

        def finish_round(s):
            add_mom(s, 0)
            precondition(s, 0, nc.gpsimd)
            add_mom(s, 1)
            multiply_upd_tile(s - 2)
            update(s - 2, 0)
            update(s - 2, 1)
            precondition(s, 1, nc.vector)

        first = 2
        turn_step(first - 2)
        empty_step(first - 2)
        widen(first + 3)
        quantize_grad(first + 1)
        quantize_step(first - 2)
        multiply_low(first)
        turn_grad(first + 2)
        empty_grad(first + 2)
        widen(first + 4)
        finish_round(first)

        for s in range(first + 1, TILES - 2):
            if s % PAIR == 0:
                if s + 4 < TILES:
                    load_grad(s + 4, PAIR)
                load_mom_pre(s + 2, PAIR)
                load_w(s, PAIR)
            turn_grad(s + 2)
            turn_step(s - 2)
            empty_step(s - 2)
            empty_grad(s + 2)
            if s + 3 < TILES:
                split_words(s + 3)
            if s + 4 < TILES:
                widen(s + 4)
            update(s - 3, 2)
            quantize_grad(s + 1)
            quantize_step(s - 2)
            multiply_low(s)
            finish_round(s)

        a, b, c, d = range(TILES - 4, TILES)
        load_w(c, PAIR)
        turn_step(a, 2)
        turn_step(b, 0)
        empty_step(a)
        empty_step(b)
        quantize_grad(d)
        quantize_step(a)
        update(a - 1, 2)
        multiply_low(c, (3, 4))
        add_mom(c, 0)
        precondition(c, 0, nc.gpsimd)
        add_mom(c, 1)
        multiply_upd(a, 0, 5)
        multiply_upd(a, 1, 6)
        multiply_low(d, (1, 2))
        update(a, 0)
        update(a, 1)
        quantize_step(b)
        add_mom(d, 0)
        precondition(c, 1, nc.vector)
        precondition(d, 0, nc.gpsimd)
        multiply_upd(a, 2, 7)
        add_mom(d, 1)
        update(a, 2)
        multiply_upd(b, 0, 3)
        turn_step(c, 0)
        empty_step(c)
        update(b, 0)
        precondition(d, 1, nc.vector)
        multiply_upd(b, 1, 4)
        multiply_upd(b, 2, 5)
        turn_step(d, 6)
        empty_step(d)
        quantize_step(c)
        multiply_upd_tile(c, (1, 2, 7))
        update(b, 1)
        update(b, 2)
        quantize_step(d)
        multiply_upd_tile(d, (0, 3, 4))
        for i in (c, d):
            for n in range(K_BANKS):
                update(i, n)
